import numpy as np, ml_dtypes
CORES = [30,158,46,174,86,214]
N = 6
C = 128
def setup_inputs(rng):
    x = 150 * rng.standard_normal((1, 128, C), dtype=np.float32) + 2 * rng.standard_normal((N, 128, C), dtype=np.float32)
    x = (x + rng.uniform(100, 300, (1, 128, C)) * (rng.random((1, 128, C)) < 0.7) * (rng.random((N, 128, C)) < 0.5)).astype(np.float32)
    return {"x": x}
def setup_inputs_trail(rng):
    d = setup_inputs(rng); x = d["x"].copy(); t = int(rng.integers(N))
    x[t] = np.delete(x, t, axis=0).max(axis=0) - rng.uniform(3.0, 20.0, x[t].shape).astype(np.float32)
    return {"x": x}
def reference(x):
    X = x.astype(np.float64)
    P = np.exp(X - X.max(axis=0))
    return {"y": (P / P.sum(axis=0)).astype(ml_dtypes.bfloat16)}

@@ -1,0 +1,83 @@
+from concourse.bass import DstId, RemoteDMATransfer
+from concourse.mybir import AluOpType, ActivationFunctionType
+
+N = 6
+C = 128
+CLAMP = 60.0
+
+SCRATCH = {
+    "land": ("sbuf", [128, N * C], "float32"),
+    "d": ("sbuf", [128, (N - 1) * C], "float32"),
+    "q": ("sbuf", [128, (N - 1) * C], "float32"),
+    "rc": ("sbuf", [128, C], "float32"),
+    "yb": ("sbuf", [128, C], "bfloat16"),
+    "xp": ("psum", [128, 512], "float32"),
+    "acc": ("psum", [128, 512], "float32"),
+}
+SEMAPHORES = (["ld", "sent", "st", "xpc", "rcp", "cst"]
+              + ["arr%d" % s for s in range(N)]
+              + ["%s%d" % (n, k) for n in ("sd", "su", "sq", "sa") for k in range(1, N)])
+
+
+def rank_program(g, core, T, topo):
+    r = T.rank_of(core)
+    if r is None:
+        return
+    v, sc, sy = g.vector, g.scalar, g.sync
+    S = T.sem
+    own = T.land[:, r * C:(r + 1) * C]
+
+    sy.dma_start(own, T.x[:]).then_inc(S.ld, 16)
+
+    dests = [T.cores[(r + k) % N] for k in range(1, N)]
+    mask = topo.mask(core, dests[0])
+    for dcore in dests:
+        mask &= topo.mask(core, dcore)
+    eng = bin(mask).count("1")
+    ids = []
+    for dcore in dests:
+        rid, pid = topo.addr(dcore, core)
+        ids.append(DstId(rid=rid, pnc=pid))
+    g.wait_ge(S.ld, 16)
+    g.remote_dma_fused(
+        [RemoteDMATransfer(dst_ids=ids, dma_engine_mask=mask, remote_sem=S["arr%d" % r],
+                           srcs=[own], dsts=[own] * len(dests), alu_op=0)],
+        local_sem=S.sent)
+
+    xp = T.xp[:, 0:C]
+    acc = T.acc[:, 0:C]
+    v.wait_ge(S.ld, 16)
+    v.tensor_copy(xp, own).then_inc(S.xpc, 1)
+    v.wait_ge(S.xpc, 1)
+
+    def blk(buf, k):
+        return buf[:, (k - 1) * C:k * C]
+
+    def add(k):
+        v.wait_ge(S["sq%d" % k], 1)
+        if k == 1:
+            v.tensor_scalar(acc, blk(T.q, k), 1.0, None, AluOpType.add).then_inc(S["sa%d" % k], 1)
+        else:
+            v.wait_ge(S["sa%d" % (k - 1)], 1)
+            v.tensor_tensor(acc, acc, blk(T.q, k), AluOpType.add).then_inc(S["sa%d" % k], 1)
+
+    for k in range(1, N):
+        s = (r - k) % N
+        v.wait_ge(S["arr%d" % s], eng)
+        v.tensor_tensor(blk(T.d, k), T.land[:, s * C:(s + 1) * C], xp, AluOpType.subtract).then_inc(S["sd%d" % k], 1)
+        sc.wait_ge(S["sd%d" % k], 1)
+        sc.activation(blk(T.d, k), blk(T.d, k), ActivationFunctionType.Relu, bias=CLAMP, scale=-1.0).then_inc(S["su%d" % k], 1)
+        sc.wait_ge(S["su%d" % k], 1)
+        sc.activation(blk(T.q, k), blk(T.d, k), ActivationFunctionType.Exp, bias=CLAMP, scale=-1.0).then_inc(S["sq%d" % k], 1)
+        if k > 1:
+            add(k - 1)
+    add(N - 1)
+    v.wait_ge(S["sa%d" % (N - 1)], 1)
+    v.reciprocal(T.rc[:], acc).then_inc(S.rcp, 1)
+    v.wait_ge(S.rcp, 1)
+    v.tensor_copy(T.yb[:], T.rc[:]).then_inc(S.cst, 1)
+
+    sy.wait_ge(S.cst, 1)
+    sy.dma_start(T.y[:], T.yb[:]).then_inc(S.st, 16)
+    sy.wait_ge(S.st, 16)
+    g.wait_ge(S.sent, eng)

@@ -3,76 +3,132 @@ from concourse.mybir import AluOpType, ActivationFunctionType
 
 N = 6
 C = 128
+H = C // 2
 CLAMP = 60.0
+NCORES = 256
+NDIRECT = 3
 
 SCRATCH = {
+    "xd": ("dram", [128, C], "float32"),
+    "hx": ("dram", [128, C], "float32"),
     "land": ("sbuf", [128, N * C], "float32"),
     "d": ("sbuf", [128, (N - 1) * C], "float32"),
-    "q": ("sbuf", [128, (N - 1) * C], "float32"),
+    "q": ("sbuf", [128, N * C], "bfloat16"),
+    "ones": ("sbuf", [128, C], "bfloat16"),
+    "ident": ("sbuf", [128, C], "bfloat16"),
     "rc": ("sbuf", [128, C], "float32"),
     "yb": ("sbuf", [128, C], "bfloat16"),
     "xp": ("psum", [128, 512], "float32"),
     "acc": ("psum", [128, 512], "float32"),
 }
-SEMAPHORES = (["ld", "sent", "st", "xpc", "rcp", "cst"]
+SEMAPHORES = (["ld", "ldd", "sent", "st", "xpc", "rcp", "cst", "hin", "one", "idn", "sum", "sq0"]
               + ["arr%d" % s for s in range(N)]
-              + ["%s%d" % (n, k) for n in ("sd", "su", "sq", "sa") for k in range(1, N)])
+              + ["%s%d" % (n, k) for n in ("sd", "sm", "su", "sq") for k in range(1, N)])
+
+
+def plan(T, topo, r):
+    rc = T.cores[r]
+    dests = [T.cores[(r + k) % N] for k in range(1, N)]
+    direct, relayed = dests[:NDIRECT], dests[NDIRECT:]
+    relay = [c for c in range(NCORES)
+             if topo.host(c) == topo.host(rc) and topo.chip(c) == topo.chip(rc) and topo.die(c) != topo.die(rc)
+             and c not in T.cores and all(topo.may_write(c, dc) for dc in relayed)][0]
+    return direct, relayed, relay
+
+
+def common_mask(topo, core, dests):
+    mask = topo.mask(core, dests[0])
+    for dc in dests:
+        mask &= topo.mask(core, dc)
+    return mask
+
+
+def ids_of(topo, core, dests):
+    out = []
+    for dc in dests:
+        rid, pid = topo.addr(dc, core)
+        out.append(DstId(rid=rid, pnc=pid))
+    return out
 
 
 def rank_program(g, core, T, topo):
+    S = T.sem
     r = T.rank_of(core)
     if r is None:
+        for rr in range(N):
+            direct, relayed, relay = plan(T, topo, rr)
+            if relay != core:
+                continue
+            rc = T.cores[rr]
+            n_in = bin(topo.mask(rc, core) & ~common_mask(topo, rc, direct)).count("1")
+            mask = common_mask(topo, core, relayed)
+            slot = T.land[:, rr * C:(rr + 1) * C]
+            g.wait_ge(S.hin, n_in)
+            g.remote_dma_fused(
+                [RemoteDMATransfer(dst_ids=ids_of(topo, core, relayed), dma_engine_mask=mask,
+                                   remote_sem=S["arr%d" % rr], srcs=[T.hx[:]], dsts=[slot] * len(relayed), alu_op=0)],
+                local_sem=S.sent)
+            g.wait_ge(S.sent, bin(mask).count("1"))
         return
-    v, sc, sy = g.vector, g.scalar, g.sync
-    S = T.sem
+
+    v, sc, sy, te = g.vector, g.scalar, g.sync, g.tensor
+    Act = ActivationFunctionType
     own = T.land[:, r * C:(r + 1) * C]
+    direct, relayed, relay = plan(T, topo, r)
 
-    sy.dma_start(own, T.x[:]).then_inc(S.ld, 16)
+    sy.dma_start(T.xd[:], T.x[:]).then_inc(S.ldd, 16)
+    sc.dma_start(own, T.x[:]).then_inc(S.ld, 16)
+    v.memset(T.ones[:], 1.0).then_inc(S.one, 1)
 
-    dests = [T.cores[(r + k) % N] for k in range(1, N)]
-    mask = topo.mask(core, dests[0])
-    for dcore in dests:
-        mask &= topo.mask(core, dcore)
-    eng = bin(mask).count("1")
-    ids = []
-    for dcore in dests:
-        rid, pid = topo.addr(dcore, core)
-        ids.append(DstId(rid=rid, pnc=pid))
-    g.wait_ge(S.ld, 16)
+    off = common_mask(topo, core, direct)
+    on = topo.mask(core, relay) & ~off
+    eng = bin(off).count("1")
+    g.wait_ge(S.ldd, 16)
     g.remote_dma_fused(
-        [RemoteDMATransfer(dst_ids=ids, dma_engine_mask=mask, remote_sem=S["arr%d" % r],
-                           srcs=[own], dsts=[own] * len(dests), alu_op=0)],
+        [RemoteDMATransfer(dst_ids=ids_of(topo, core, [relay]), dma_engine_mask=on, remote_sem=S.hin,
+                           srcs=[T.xd[:]], dsts=[T.hx[:]], alu_op=0),
+         RemoteDMATransfer(dst_ids=ids_of(topo, core, direct), dma_engine_mask=off, remote_sem=S["arr%d" % r],
+                           srcs=[T.xd[:]], dsts=[own] * len(direct), alu_op=0)],
         local_sem=S.sent)
+    g.wait_ge(S.one, 1)
+    g.affine_select(T.ident[:], T.ones[:], [[-1, C]], AluOpType.is_equal, 0.0, 0, 1).then_inc(S.idn, 1)
 
     xp = T.xp[:, 0:C]
     acc = T.acc[:, 0:C]
+
+    def blk(buf, k):
+        return buf[:, k * C:(k + 1) * C]
+
     v.wait_ge(S.ld, 16)
     v.tensor_copy(xp, own).then_inc(S.xpc, 1)
     v.wait_ge(S.xpc, 1)
-
-    def blk(buf, k):
-        return buf[:, (k - 1) * C:k * C]
-
-    def add(k):
-        v.wait_ge(S["sq%d" % k], 1)
-        if k == 1:
-            v.tensor_scalar(acc, blk(T.q, k), 1.0, None, AluOpType.add).then_inc(S["sa%d" % k], 1)
-        else:
-            v.wait_ge(S["sa%d" % (k - 1)], 1)
-            v.tensor_tensor(acc, acc, blk(T.q, k), AluOpType.add).then_inc(S["sa%d" % k], 1)
+    sc.wait_ge(S.ld, 16)
+    sc.activation(blk(T.q, 0), own, Act.Exp, bias=0.0, scale=0.0).then_inc(S.sq0, 1)
+    te.wait_ge(S.idn, 1)
+    te.wait_ge(S.sq0, 1)
+    te.matmul(acc, T.ident[:], blk(T.q, 0), True, False)
 
     for k in range(1, N):
         s = (r - k) % N
+        dk = blk(T.d, k - 1)
+        qk = blk(T.q, k)
+        sd, sm, su, sq = S["sd%d" % k], S["sm%d" % k], S["su%d" % k], S["sq%d" % k]
         v.wait_ge(S["arr%d" % s], eng)
-        v.tensor_tensor(blk(T.d, k), T.land[:, s * C:(s + 1) * C], xp, AluOpType.subtract).then_inc(S["sd%d" % k], 1)
-        sc.wait_ge(S["sd%d" % k], 1)
-        sc.activation(blk(T.d, k), blk(T.d, k), ActivationFunctionType.Relu, bias=CLAMP, scale=-1.0).then_inc(S["su%d" % k], 1)
-        sc.wait_ge(S["su%d" % k], 1)
-        sc.activation(blk(T.q, k), blk(T.d, k), ActivationFunctionType.Exp, bias=CLAMP, scale=-1.0).then_inc(S["sq%d" % k], 1)
-        if k > 1:
-            add(k - 1)
-    add(N - 1)
-    v.wait_ge(S["sa%d" % (N - 1)], 1)
+        v.tensor_tensor(dk, blk(T.land, s), xp, AluOpType.subtract).then_inc(sd, 1)
+        v.wait_ge(sd, 1)
+        v.tensor_scalar(dk[:, 0:H], dk[:, 0:H], CLAMP, None, AluOpType.min).then_inc(sm, 1)
+        sc.wait_ge(sd, 1)
+        sc.activation(dk[:, H:C], dk[:, H:C], Act.Relu, bias=CLAMP, scale=-1.0).then_inc(su, 1)
+        sc.wait_ge(su, 1)
+        sc.activation(qk[:, H:C], dk[:, H:C], Act.Exp, bias=CLAMP, scale=-1.0).then_inc(sq, 1)
+        sc.wait_ge(sm, 1)
+        sc.activation(qk[:, 0:H], dk[:, 0:H], Act.Exp).then_inc(sq, 1)
+        te.wait_ge(sq, 2)
+        mm = te.matmul(acc, T.ident[:], qk, False, k == N - 1)
+        if k == N - 1:
+            mm.then_inc(S.sum, 1)
+
+    v.wait_ge(S.sum, 1)
     v.reciprocal(T.rc[:], acc).then_inc(S.rcp, 1)
     v.wait_ge(S.rcp, 1)
     v.tensor_copy(T.yb[:], T.rc[:]).then_inc(S.cst, 1)
@@ -80,4 +136,4 @@ def rank_program(g, core, T, topo):
     sy.wait_ge(S.cst, 1)
     sy.dma_start(T.y[:], T.yb[:]).then_inc(S.st, 16)
     sy.wait_ge(S.st, 16)
-    g.wait_ge(S.sent, eng)
+    g.wait_ge(S.sent, eng + bin(on).count("1"))

@@ -6,7 +6,8 @@ C = 128
 H = C // 2
 CLAMP = 60.0
 NCORES = 256
-NDIRECT = 3
+SHARE = (2, 2, 1)
+ORDER = (1, 2, 3, 5, 4)
 
 SCRATCH = {
     "xd": ("dram", [128, C], "float32"),
@@ -14,26 +15,33 @@ SCRATCH = {
     "land": ("sbuf", [128, N * C], "float32"),
     "d": ("sbuf", [128, (N - 1) * C], "float32"),
     "q": ("sbuf", [128, N * C], "bfloat16"),
-    "ones": ("sbuf", [128, C], "bfloat16"),
+    "z": ("sbuf", [128, C], "bfloat16"),
+    "ones": ("sbuf", [128, H], "bfloat16"),
     "ident": ("sbuf", [128, C], "bfloat16"),
     "rc": ("sbuf", [128, C], "float32"),
     "yb": ("sbuf", [128, C], "bfloat16"),
     "xp": ("psum", [128, 512], "float32"),
     "acc": ("psum", [128, 512], "float32"),
 }
-SEMAPHORES = (["ld", "ldd", "sent", "st", "xpc", "rcp", "cst", "hin", "one", "idn", "sum", "sq0"]
+SEMAPHORES = (["ld", "ldd", "sent", "st", "xpc", "rcp", "cst", "hin", "one", "idm", "idn", "sum", "sq0", "zf"]
               + ["arr%d" % s for s in range(N)]
-              + ["%s%d" % (n, k) for n in ("sd", "sm", "su", "sq") for k in range(1, N)])
+              + ["%s%d" % (n, k) for n in ("sda", "sdb", "sm", "su", "sqa", "sqb") for k in range(1, N)])
 
 
 def plan(T, topo, r):
     rc = T.cores[r]
     dests = [T.cores[(r + k) % N] for k in range(1, N)]
-    direct, relayed = dests[:NDIRECT], dests[NDIRECT:]
-    relay = [c for c in range(NCORES)
-             if topo.host(c) == topo.host(rc) and topo.chip(c) == topo.chip(rc) and topo.die(c) != topo.die(rc)
-             and c not in T.cores and all(topo.may_write(c, dc) for dc in relayed)][0]
-    return direct, relayed, relay
+    parts, at = [], 0
+    for n in SHARE:
+        parts.append(dests[at:at + n])
+        at += n
+    out = [(rc, parts[0])]
+    for part, other_die in ((parts[1], True), (parts[2], False)):
+        c = [c for c in range(NCORES)
+             if topo.host(c) == topo.host(rc) and topo.chip(c) == topo.chip(rc) and c not in T.cores
+             and (topo.die(c) != topo.die(rc)) == other_die and all(topo.may_write(c, dc) for dc in part)][0]
+        out.append((c, part))
+    return out
 
 
 def common_mask(topo, core, dests):
@@ -51,47 +59,73 @@ def ids_of(topo, core, dests):
     return out
 
 
+def bits(mask):
+    return bin(mask).count("1")
+
+
+def fan_mask(topo, p):
+    rc = p[0][0]
+    return common_mask(topo, rc, [p[1][0], p[2][0]]) & ~common_mask(topo, rc, p[0][1])
+
+
+def relay_program(g, core, T, topo, rr, p, part):
+    S = T.sem
+    rc = p[0][0]
+    dests = p[1 + part][1]
+    mask = common_mask(topo, core, dests)
+    half = T.ident[:, part * H:(part + 1) * H]
+    g.vector.memset(T.ones[:], 1.0).then_inc(S.one, 1)
+    g.wait_ge(S.one, 1)
+    g.affine_select(half, T.ones[:], [[-1, H]], AluOpType.is_equal, 0.0, -part * H, 1).then_inc(S.idm, 1)
+    g.wait_ge(S.idm, 1)
+    g.remote_dma_fused(
+        [RemoteDMATransfer(dst_ids=ids_of(topo, core, [rc]), dma_engine_mask=mask, remote_sem=S.idn,
+                           srcs=[half], dsts=[half], alu_op=0)],
+        local_sem=S.sent)
+    slot = T.land[:, rr * C:(rr + 1) * C]
+    g.wait_ge(S.hin, bits(fan_mask(topo, p)))
+    g.remote_dma_fused(
+        [RemoteDMATransfer(dst_ids=ids_of(topo, core, dests), dma_engine_mask=mask, remote_sem=S["arr%d" % rr],
+                           srcs=[T.hx[:]], dsts=[slot] * len(dests), alu_op=0)],
+        local_sem=S.sent)
+    g.wait_ge(S.sent, 2 * bits(mask))
+
+
 def rank_program(g, core, T, topo):
     S = T.sem
     r = T.rank_of(core)
     if r is None:
         for rr in range(N):
-            direct, relayed, relay = plan(T, topo, rr)
-            if relay != core:
-                continue
-            rc = T.cores[rr]
-            n_in = bin(topo.mask(rc, core) & ~common_mask(topo, rc, direct)).count("1")
-            mask = common_mask(topo, core, relayed)
-            slot = T.land[:, rr * C:(rr + 1) * C]
-            g.wait_ge(S.hin, n_in)
-            g.remote_dma_fused(
-                [RemoteDMATransfer(dst_ids=ids_of(topo, core, relayed), dma_engine_mask=mask,
-                                   remote_sem=S["arr%d" % rr], srcs=[T.hx[:]], dsts=[slot] * len(relayed), alu_op=0)],
-                local_sem=S.sent)
-            g.wait_ge(S.sent, bin(mask).count("1"))
+            p = plan(T, topo, rr)
+            for part in (0, 1):
+                if p[1 + part][0] == core:
+                    relay_program(g, core, T, topo, rr, p, part)
         return
 
     v, sc, sy, te = g.vector, g.scalar, g.sync, g.tensor
     Act = ActivationFunctionType
     own = T.land[:, r * C:(r + 1) * C]
-    direct, relayed, relay = plan(T, topo, r)
+    p = plan(T, topo, r)
+    direct = p[0][1]
+    relays = [p[1][0], p[2][0]]
 
     sy.dma_start(T.xd[:], T.x[:]).then_inc(S.ldd, 16)
     sc.dma_start(own, T.x[:]).then_inc(S.ld, 16)
-    v.memset(T.ones[:], 1.0).then_inc(S.one, 1)
+    v.memset(T.z[:], 0.0).then_inc(S.zf, 1)
 
     off = common_mask(topo, core, direct)
-    on = topo.mask(core, relay) & ~off
-    eng = bin(off).count("1")
+    on = fan_mask(topo, p)
     g.wait_ge(S.ldd, 16)
     g.remote_dma_fused(
-        [RemoteDMATransfer(dst_ids=ids_of(topo, core, [relay]), dma_engine_mask=on, remote_sem=S.hin,
+        [RemoteDMATransfer(dst_ids=ids_of(topo, core, relays[0:1]), dma_engine_mask=on, remote_sem=S.hin,
                            srcs=[T.xd[:]], dsts=[T.hx[:]], alu_op=0),
          RemoteDMATransfer(dst_ids=ids_of(topo, core, direct), dma_engine_mask=off, remote_sem=S["arr%d" % r],
                            srcs=[T.xd[:]], dsts=[own] * len(direct), alu_op=0)],
         local_sem=S.sent)
-    g.wait_ge(S.one, 1)
-    g.affine_select(T.ident[:], T.ones[:], [[-1, C]], AluOpType.is_equal, 0.0, 0, 1).then_inc(S.idn, 1)
+    g.remote_dma_fused(
+        [RemoteDMATransfer(dst_ids=ids_of(topo, core, relays[1:2]), dma_engine_mask=on, remote_sem=S.hin,
+                           srcs=[T.xd[:]], dsts=[T.hx[:]], alu_op=0)],
+        local_sem=S.sent)
 
     xp = T.xp[:, 0:C]
     acc = T.acc[:, 0:C]
@@ -99,41 +133,59 @@ def rank_program(g, core, T, topo):
     def blk(buf, k):
         return buf[:, k * C:(k + 1) * C]
 
+    def sem(n, k):
+        return S["%s%d" % (n, k)]
+
+    sc.wait_ge(S.zf, 1)
+    sc.activation(blk(T.q, 0), T.z[:], Act.Exp).then_inc(S.sq0, 1)
     v.wait_ge(S.ld, 16)
     v.tensor_copy(xp, own).then_inc(S.xpc, 1)
     v.wait_ge(S.xpc, 1)
-    sc.wait_ge(S.ld, 16)
-    sc.activation(blk(T.q, 0), own, Act.Exp, bias=0.0, scale=0.0).then_inc(S.sq0, 1)
-    te.wait_ge(S.idn, 1)
+    n_idn = sum(bits(common_mask(topo, c, ds)) for c, ds in p[1:])
+    te.wait_ge(S.idn, n_idn)
     te.wait_ge(S.sq0, 1)
     te.matmul(acc, T.ident[:], blk(T.q, 0), True, False)
 
-    for k in range(1, N):
+    def step1(k):
         s = (r - k) % N
-        dk = blk(T.d, k - 1)
-        qk = blk(T.q, k)
-        sd, sm, su, sq = S["sd%d" % k], S["sm%d" % k], S["su%d" % k], S["sq%d" % k]
-        v.wait_ge(S["arr%d" % s], eng)
-        v.tensor_tensor(dk, blk(T.land, s), xp, AluOpType.subtract).then_inc(sd, 1)
-        v.wait_ge(sd, 1)
-        v.tensor_scalar(dk[:, 0:H], dk[:, 0:H], CLAMP, None, AluOpType.min).then_inc(sm, 1)
-        sc.wait_ge(sd, 1)
-        sc.activation(dk[:, H:C], dk[:, H:C], Act.Relu, bias=CLAMP, scale=-1.0).then_inc(su, 1)
-        sc.wait_ge(su, 1)
-        sc.activation(qk[:, H:C], dk[:, H:C], Act.Exp, bias=CLAMP, scale=-1.0).then_inc(sq, 1)
-        sc.wait_ge(sm, 1)
-        sc.activation(qk[:, 0:H], dk[:, 0:H], Act.Exp).then_inc(sq, 1)
-        te.wait_ge(sq, 2)
-        mm = te.matmul(acc, T.ident[:], qk, False, k == N - 1)
-        if k == N - 1:
-            mm.then_inc(S.sum, 1)
+        n_arr = [bits(common_mask(topo, c, ds)) for c, ds in plan(T, topo, s) if core in ds][0]
+        xs, dk = blk(T.land, s), blk(T.d, k - 1)
+        v.wait_ge(S["arr%d" % s], n_arr)
+        v.tensor_tensor(dk[:, 0:H], xs[:, 0:H], xp[:, 0:H], AluOpType.subtract).then_inc(sem("sda", k), 1)
+        v.tensor_tensor(dk[:, H:C], xs[:, H:C], xp[:, H:C], AluOpType.subtract).then_inc(sem("sdb", k), 1)
+        sc.wait_ge(sem("sda", k), 1)
+        sc.activation(dk[:, 0:H], dk[:, 0:H], Act.Relu, bias=CLAMP, scale=-1.0).then_inc(sem("su", k), 1)
 
-    v.wait_ge(S.sum, 1)
+    def step2(k, last):
+        dk, qk = blk(T.d, k - 1), blk(T.q, k)
+        v.wait_ge(sem("sdb", k), 1)
+        v.tensor_scalar(dk[:, H:C], dk[:, H:C], CLAMP, None, AluOpType.min).then_inc(sem("sm", k), 1)
+        sc.wait_ge(sem("su", k), 1)
+        sc.activation(qk[:, 0:H], dk[:, 0:H], Act.Exp, bias=CLAMP, scale=-1.0).then_inc(sem("sqa", k), 1)
+        sc.wait_ge(sem("sm", k), 1)
+        sc.activation(qk[:, H:C], dk[:, H:C], Act.Exp).then_inc(sem("sqb", k), 1)
+        te.wait_ge(sem("sqa", k), 1)
+        ma = te.matmul(acc[:, 0:H], T.ident[:], qk[:, 0:H], False, False)
+        te.wait_ge(sem("sqb", k), 1)
+        mb = te.matmul(acc[:, H:C], T.ident[:], qk[:, H:C], False, last)
+        if last:
+            ma.then_inc(S.sum, 1)
+            mb.then_inc(S.sum, 1)
+
+    for i, k in enumerate(ORDER):
+        step1(k)
+        if i > 0:
+            step2(ORDER[i - 1], False)
+    step2(ORDER[-1], True)
+
+    v.wait_ge(S.sum, 2)
     v.reciprocal(T.rc[:], acc).then_inc(S.rcp, 1)
     v.wait_ge(S.rcp, 1)
-    v.tensor_copy(T.yb[:], T.rc[:]).then_inc(S.cst, 1)
+    v.tensor_copy(T.yb[:, 0:H], T.rc[:, 0:H]).then_inc(S.cst, 1)
+    sc.wait_ge(S.rcp, 1)
+    sc.activation(T.yb[:, H:C], T.rc[:, H:C], Act.Copy).then_inc(S.cst, 1)
 
-    sy.wait_ge(S.cst, 1)
+    sy.wait_ge(S.cst, 2)
     sy.dma_start(T.y[:], T.yb[:]).then_inc(S.st, 16)
     sy.wait_ge(S.st, 16)
-    g.wait_ge(S.sent, eng + bin(on).count("1"))
+    g.wait_ge(S.sent, bits(off) + 2 * bits(on))

@@ -8,6 +8,7 @@ CLAMP = 60.0
 NCORES = 256
 SHARE = (2, 2, 1)
 ORDER = (1, 2, 3, 5, 4)
+PARTS = ((0, 56), (56, 56), (112, 16))
 
 SCRATCH = {
     "xd": ("dram", [128, C], "float32"),
@@ -16,14 +17,14 @@ SCRATCH = {
     "d": ("sbuf", [128, (N - 1) * C], "float32"),
     "q": ("sbuf", [128, N * C], "bfloat16"),
     "z": ("sbuf", [128, C], "bfloat16"),
-    "ones": ("sbuf", [128, H], "bfloat16"),
+    "ones": ("sbuf", [128, PARTS[0][1]], "bfloat16"),
     "ident": ("sbuf", [128, C], "bfloat16"),
     "rc": ("sbuf", [128, C], "float32"),
     "yb": ("sbuf", [128, C], "bfloat16"),
     "xp": ("psum", [128, 512], "float32"),
     "acc": ("psum", [128, 512], "float32"),
 }
-SEMAPHORES = (["ld", "ldd", "sent", "st", "xpc", "rcp", "cst", "hin", "one", "idm", "idn", "sum", "sq0", "zf"]
+SEMAPHORES = (["ld", "ldd", "sent", "st", "xpc", "rcp", "cst", "hin", "ong", "one", "idm", "idn", "sum", "sq0", "zf"]
               + ["arr%d" % s for s in range(N)]
               + ["%s%d" % (n, k) for n in ("sda", "sdb", "sm", "su", "sqa", "sqb") for k in range(1, N)])
 
@@ -42,6 +43,14 @@ def plan(T, topo, r):
              and (topo.die(c) != topo.die(rc)) == other_die and all(topo.may_write(c, dc) for dc in part)][0]
         out.append((c, part))
     return out
+
+
+def helper(T, topo, p):
+    rc = p[0][0]
+    used = [c for c, _ in p]
+    return [c for c in range(NCORES)
+            if topo.host(c) == topo.host(rc) and topo.chip(c) == topo.chip(rc) and topo.die(c) == topo.die(rc)
+            and c not in T.cores and c not in used and topo.may_write(c, rc) and topo.may_write(rc, c)][0]
 
 
 def common_mask(topo, core, dests):
@@ -63,9 +72,26 @@ def bits(mask):
     return bin(mask).count("1")
 
 
+def first_engines(mask, k):
+    out = 0
+    for b in range(mask.bit_length()):
+        if (mask >> b) & 1 and bits(out) < k:
+            out |= 1 << b
+    return out
+
+
 def fan_mask(topo, p):
     rc = p[0][0]
     return common_mask(topo, rc, [p[1][0], p[2][0]]) & ~common_mask(topo, rc, p[0][1])
+
+
+def early_mask(topo, p, hd):
+    rc = p[0][0]
+    return (common_mask(topo, rc, p[0][1]) | fan_mask(topo, p)) & topo.mask(rc, hd)
+
+
+def back_mask(topo, p, hd):
+    return first_engines(topo.mask(hd, p[0][0]), 8)
 
 
 def relay_program(g, core, T, topo, rr, p, part):
@@ -73,14 +99,15 @@ def relay_program(g, core, T, topo, rr, p, part):
     rc = p[0][0]
     dests = p[1 + part][1]
     mask = common_mask(topo, core, dests)
-    half = T.ident[:, part * H:(part + 1) * H]
-    g.vector.memset(T.ones[:], 1.0).then_inc(S.one, 1)
+    c0, w = PARTS[part]
+    piece = T.ident[:, c0:c0 + w]
+    g.vector.memset(T.ones[:, 0:w], 1.0).then_inc(S.one, 1)
     g.wait_ge(S.one, 1)
-    g.affine_select(half, T.ones[:], [[-1, H]], AluOpType.is_equal, 0.0, -part * H, 1).then_inc(S.idm, 1)
+    g.affine_select(piece, T.ones[:, 0:w], [[-1, w]], AluOpType.is_equal, 0.0, -c0, 1).then_inc(S.idm, 1)
     g.wait_ge(S.idm, 1)
     g.remote_dma_fused(
         [RemoteDMATransfer(dst_ids=ids_of(topo, core, [rc]), dma_engine_mask=mask, remote_sem=S.idn,
-                           srcs=[half], dsts=[half], alu_op=0)],
+                           srcs=[piece], dsts=[piece], alu_op=0)],
         local_sem=S.sent)
     slot = T.land[:, rr * C:(rr + 1) * C]
     g.wait_ge(S.hin, bits(fan_mask(topo, p)))
@@ -89,6 +116,22 @@ def relay_program(g, core, T, topo, rr, p, part):
                            srcs=[T.hx[:]], dsts=[slot] * len(dests), alu_op=0)],
         local_sem=S.sent)
     g.wait_ge(S.sent, 2 * bits(mask))
+
+
+def helper_program(g, core, T, topo, p):
+    S = T.sem
+    rc = p[0][0]
+    c0, w = PARTS[2]
+    piece = T.ident[:, c0:c0 + w]
+    mask = back_mask(topo, p, core)
+    g.wait_ge(S.ong, bits(early_mask(topo, p, core)))
+    g.affine_select(piece, T.ones[:, 0:w], [[-1, w]], AluOpType.is_equal, 0.0, -c0, 1).then_inc(S.idm, 1)
+    g.wait_ge(S.idm, 1)
+    g.remote_dma_fused(
+        [RemoteDMATransfer(dst_ids=ids_of(topo, core, [rc]), dma_engine_mask=mask, remote_sem=S.idn,
+                           srcs=[piece], dsts=[piece], alu_op=0)],
+        local_sem=S.sent)
+    g.wait_ge(S.sent, bits(mask))
 
 
 def rank_program(g, core, T, topo):
@@ -100,6 +143,8 @@ def rank_program(g, core, T, topo):
             for part in (0, 1):
                 if p[1 + part][0] == core:
                     relay_program(g, core, T, topo, rr, p, part)
+            if helper(T, topo, p) == core:
+                helper_program(g, core, T, topo, p)
         return
 
     v, sc, sy, te = g.vector, g.scalar, g.sync, g.tensor
@@ -108,10 +153,20 @@ def rank_program(g, core, T, topo):
     p = plan(T, topo, r)
     direct = p[0][1]
     relays = [p[1][0], p[2][0]]
+    hd = helper(T, topo, p)
+    wd = PARTS[2][1]
 
     sy.dma_start(T.xd[:], T.x[:]).then_inc(S.ldd, 16)
     sc.dma_start(own, T.x[:]).then_inc(S.ld, 16)
+    v.memset(T.ones[:, 0:wd], 1.0).then_inc(S.one, 1)
     v.memset(T.z[:], 0.0).then_inc(S.zf, 1)
+
+    early = early_mask(topo, p, hd)
+    g.wait_ge(S.one, 1)
+    g.remote_dma_fused(
+        [RemoteDMATransfer(dst_ids=ids_of(topo, core, [hd]), dma_engine_mask=early, remote_sem=S.ong,
+                           srcs=[T.ones[:, 0:wd]], dsts=[T.ones[:, 0:wd]], alu_op=0)],
+        local_sem=S.sent)
 
     off = common_mask(topo, core, direct)
     on = fan_mask(topo, p)
@@ -141,7 +196,7 @@ def rank_program(g, core, T, topo):
     v.wait_ge(S.ld, 16)
     v.tensor_copy(xp, own).then_inc(S.xpc, 1)
     v.wait_ge(S.xpc, 1)
-    n_idn = sum(bits(common_mask(topo, c, ds)) for c, ds in p[1:])
+    n_idn = sum(bits(common_mask(topo, c, ds)) for c, ds in p[1:]) + bits(back_mask(topo, p, hd))
     te.wait_ge(S.idn, n_idn)
     te.wait_ge(S.sq0, 1)
     te.matmul(acc, T.ident[:], blk(T.q, 0), True, False)
@@ -188,4 +243,4 @@ def rank_program(g, core, T, topo):
     sy.wait_ge(S.cst, 2)
     sy.dma_start(T.y[:], T.yb[:]).then_inc(S.st, 16)
     sy.wait_ge(S.st, 16)
-    g.wait_ge(S.sent, bits(off) + 2 * bits(on))
+    g.wait_ge(S.sent, bits(early) + bits(off) + 2 * bits(on))

from concourse.bass import DstId, RemoteDMATransfer
from concourse.mybir import AluOpType, ActivationFunctionType

N = 6
C = 128
H = C // 2
CLAMP = 60.0
NCORES = 256
SHARE = (2, 2, 1)
ORDER = (1, 2, 3, 5, 4)
PARTS = ((0, 56), (56, 56), (112, 16))

SCRATCH = {
    "xd": ("dram", [128, C], "float32"),
    "hx": ("dram", [128, C], "float32"),
    "land": ("sbuf", [128, N * C], "float32"),
    "d": ("sbuf", [128, (N - 1) * C], "float32"),
    "q": ("sbuf", [128, N * C], "bfloat16"),
    "z": ("sbuf", [128, C], "bfloat16"),
    "ones": ("sbuf", [128, PARTS[0][1]], "bfloat16"),
    "ident": ("sbuf", [128, C], "bfloat16"),
    "rc": ("sbuf", [128, C], "float32"),
    "yb": ("sbuf", [128, C], "bfloat16"),
    "xp": ("psum", [128, 512], "float32"),
    "acc": ("psum", [128, 512], "float32"),
}
SEMAPHORES = (["ld", "ldd", "sent", "st", "xpc", "rcp", "cst", "hin", "ong", "one", "idm", "idn", "sum", "sq0", "zf"]
              + ["arr%d" % s for s in range(N)]
              + ["%s%d" % (n, k) for n in ("sda", "sdb", "sm", "su", "sqa", "sqb") for k in range(1, N)])


def plan(T, topo, r):
    rc = T.cores[r]
    dests = [T.cores[(r + k) % N] for k in range(1, N)]
    parts, at = [], 0
    for n in SHARE:
        parts.append(dests[at:at + n])
        at += n
    out = [(rc, parts[0])]
    for part, other_die in ((parts[1], True), (parts[2], False)):
        c = [c for c in range(NCORES)
             if topo.host(c) == topo.host(rc) and topo.chip(c) == topo.chip(rc) and c not in T.cores
             and (topo.die(c) != topo.die(rc)) == other_die and all(topo.may_write(c, dc) for dc in part)][0]
        out.append((c, part))
    return out


def helper(T, topo, p):
    rc = p[0][0]
    used = [c for c, _ in p]
    return [c for c in range(NCORES)
            if topo.host(c) == topo.host(rc) and topo.chip(c) == topo.chip(rc) and topo.die(c) == topo.die(rc)
            and c not in T.cores and c not in used and topo.may_write(c, rc) and topo.may_write(rc, c)][0]


def common_mask(topo, core, dests):
    mask = topo.mask(core, dests[0])
    for dc in dests:
        mask &= topo.mask(core, dc)
    return mask


def ids_of(topo, core, dests):
    out = []
    for dc in dests:
        rid, pid = topo.addr(dc, core)
        out.append(DstId(rid=rid, pnc=pid))
    return out


def bits(mask):
    return bin(mask).count("1")


def first_engines(mask, k):
    out = 0
    for b in range(mask.bit_length()):
        if (mask >> b) & 1 and bits(out) < k:
            out |= 1 << b
    return out


def fan_mask(topo, p):
    rc = p[0][0]
    return common_mask(topo, rc, [p[1][0], p[2][0]]) & ~common_mask(topo, rc, p[0][1])


def early_mask(topo, p, hd):
    rc = p[0][0]
    return (common_mask(topo, rc, p[0][1]) | fan_mask(topo, p)) & topo.mask(rc, hd)


def back_mask(topo, p, hd):
    return first_engines(topo.mask(hd, p[0][0]), 8)


def relay_program(g, core, T, topo, rr, p, part):
    S = T.sem
    rc = p[0][0]
    dests = p[1 + part][1]
    mask = common_mask(topo, core, dests)
    c0, w = PARTS[part]
    piece = T.ident[:, c0:c0 + w]
    g.vector.memset(T.ones[:, 0:w], 1.0).then_inc(S.one, 1)
    g.wait_ge(S.one, 1)
    g.affine_select(piece, T.ones[:, 0:w], [[-1, w]], AluOpType.is_equal, 0.0, -c0, 1).then_inc(S.idm, 1)
    g.wait_ge(S.idm, 1)
    g.remote_dma_fused(
        [RemoteDMATransfer(dst_ids=ids_of(topo, core, [rc]), dma_engine_mask=mask, remote_sem=S.idn,
                           srcs=[piece], dsts=[piece], alu_op=0)],
        local_sem=S.sent)
    slot = T.land[:, rr * C:(rr + 1) * C]
    g.wait_ge(S.hin, bits(fan_mask(topo, p)))
    g.remote_dma_fused(
        [RemoteDMATransfer(dst_ids=ids_of(topo, core, dests), dma_engine_mask=mask, remote_sem=S["arr%d" % rr],
                           srcs=[T.hx[:]], dsts=[slot] * len(dests), alu_op=0)],
        local_sem=S.sent)
    g.wait_ge(S.sent, 2 * bits(mask))


def helper_program(g, core, T, topo, p):
    S = T.sem
    rc = p[0][0]
    c0, w = PARTS[2]
    piece = T.ident[:, c0:c0 + w]
    mask = back_mask(topo, p, core)
    g.wait_ge(S.ong, bits(early_mask(topo, p, core)))
    g.affine_select(piece, T.ones[:, 0:w], [[-1, w]], AluOpType.is_equal, 0.0, -c0, 1).then_inc(S.idm, 1)
    g.wait_ge(S.idm, 1)
    g.remote_dma_fused(
        [RemoteDMATransfer(dst_ids=ids_of(topo, core, [rc]), dma_engine_mask=mask, remote_sem=S.idn,
                           srcs=[piece], dsts=[piece], alu_op=0)],
        local_sem=S.sent)
    g.wait_ge(S.sent, bits(mask))


def rank_program(g, core, T, topo):
    S = T.sem
    r = T.rank_of(core)
    if r is None:
        for rr in range(N):
            p = plan(T, topo, rr)
            for part in (0, 1):
                if p[1 + part][0] == core:
                    relay_program(g, core, T, topo, rr, p, part)
            if helper(T, topo, p) == core:
                helper_program(g, core, T, topo, p)
        return

    v, sc, sy, te = g.vector, g.scalar, g.sync, g.tensor
    Act = ActivationFunctionType
    own = T.land[:, r * C:(r + 1) * C]
    p = plan(T, topo, r)
    direct = p[0][1]
    relays = [p[1][0], p[2][0]]
    hd = helper(T, topo, p)
    wd = PARTS[2][1]

    sy.dma_start(T.xd[:], T.x[:]).then_inc(S.ldd, 16)
    sc.dma_start(own, T.x[:]).then_inc(S.ld, 16)
    v.memset(T.ones[:, 0:wd], 1.0).then_inc(S.one, 1)
    v.memset(T.z[:], 0.0).then_inc(S.zf, 1)

    early = early_mask(topo, p, hd)
    g.wait_ge(S.one, 1)
    g.remote_dma_fused(
        [RemoteDMATransfer(dst_ids=ids_of(topo, core, [hd]), dma_engine_mask=early, remote_sem=S.ong,
                           srcs=[T.ones[:, 0:wd]], dsts=[T.ones[:, 0:wd]], alu_op=0)],
        local_sem=S.sent)

    off = common_mask(topo, core, direct)
    on = fan_mask(topo, p)
    g.wait_ge(S.ldd, 16)
    g.remote_dma_fused(
        [RemoteDMATransfer(dst_ids=ids_of(topo, core, relays[0:1]), dma_engine_mask=on, remote_sem=S.hin,
                           srcs=[T.xd[:]], dsts=[T.hx[:]], alu_op=0),
         RemoteDMATransfer(dst_ids=ids_of(topo, core, direct), dma_engine_mask=off, remote_sem=S["arr%d" % r],
                           srcs=[T.xd[:]], dsts=[own] * len(direct), alu_op=0)],
        local_sem=S.sent)
    g.remote_dma_fused(
        [RemoteDMATransfer(dst_ids=ids_of(topo, core, relays[1:2]), dma_engine_mask=on, remote_sem=S.hin,
                           srcs=[T.xd[:]], dsts=[T.hx[:]], alu_op=0)],
        local_sem=S.sent)

    xp = T.xp[:, 0:C]
    acc = T.acc[:, 0:C]

    def blk(buf, k):
        return buf[:, k * C:(k + 1) * C]

    def sem(n, k):
        return S["%s%d" % (n, k)]

    sc.wait_ge(S.zf, 1)
    sc.activation(blk(T.q, 0), T.z[:], Act.Exp).then_inc(S.sq0, 1)
    v.wait_ge(S.ld, 16)
    v.tensor_copy(xp, own).then_inc(S.xpc, 1)
    v.wait_ge(S.xpc, 1)
    n_idn = sum(bits(common_mask(topo, c, ds)) for c, ds in p[1:]) + bits(back_mask(topo, p, hd))
    te.wait_ge(S.idn, n_idn)
    te.wait_ge(S.sq0, 1)
    te.matmul(acc, T.ident[:], blk(T.q, 0), True, False)

    def step1(k):
        s = (r - k) % N
        n_arr = [bits(common_mask(topo, c, ds)) for c, ds in plan(T, topo, s) if core in ds][0]
        xs, dk = blk(T.land, s), blk(T.d, k - 1)
        v.wait_ge(S["arr%d" % s], n_arr)
        v.tensor_tensor(dk[:, 0:H], xs[:, 0:H], xp[:, 0:H], AluOpType.subtract).then_inc(sem("sda", k), 1)
        v.tensor_tensor(dk[:, H:C], xs[:, H:C], xp[:, H:C], AluOpType.subtract).then_inc(sem("sdb", k), 1)
        sc.wait_ge(sem("sda", k), 1)
        sc.activation(dk[:, 0:H], dk[:, 0:H], Act.Relu, bias=CLAMP, scale=-1.0).then_inc(sem("su", k), 1)

    def step2(k, last):
        dk, qk = blk(T.d, k - 1), blk(T.q, k)
        v.wait_ge(sem("sdb", k), 1)
        v.tensor_scalar(dk[:, H:C], dk[:, H:C], CLAMP, None, AluOpType.min).then_inc(sem("sm", k), 1)
        sc.wait_ge(sem("su", k), 1)
        sc.activation(qk[:, 0:H], dk[:, 0:H], Act.Exp, bias=CLAMP, scale=-1.0).then_inc(sem("sqa", k), 1)
        sc.wait_ge(sem("sm", k), 1)
        sc.activation(qk[:, H:C], dk[:, H:C], Act.Exp).then_inc(sem("sqb", k), 1)
        te.wait_ge(sem("sqa", k), 1)
        ma = te.matmul(acc[:, 0:H], T.ident[:], qk[:, 0:H], False, False)
        te.wait_ge(sem("sqb", k), 1)
        mb = te.matmul(acc[:, H:C], T.ident[:], qk[:, H:C], False, last)
        if last:
            ma.then_inc(S.sum, 1)
            mb.then_inc(S.sum, 1)

    for i, k in enumerate(ORDER):
        step1(k)
        if i > 0:
            step2(ORDER[i - 1], False)
    step2(ORDER[-1], True)

    v.wait_ge(S.sum, 2)
    v.reciprocal(T.rc[:], acc).then_inc(S.rcp, 1)
    v.wait_ge(S.rcp, 1)
    v.tensor_copy(T.yb[:, 0:H], T.rc[:, 0:H]).then_inc(S.cst, 1)
    sc.wait_ge(S.rcp, 1)
    sc.activation(T.yb[:, H:C], T.rc[:, H:C], Act.Copy).then_inc(S.cst, 1)

    sy.wait_ge(S.cst, 2)
    sy.dma_start(T.y[:], T.yb[:]).then_inc(S.st, 16)
    sy.wait_ge(S.st, 16)
    g.wait_ge(S.sent, bits(early) + bits(off) + 2 * bits(on))
